import numpy as np
import ml_dtypes


def mxq(x, axis, fmt="e4m3"):
    dtype, down = {"e4m3": (ml_dtypes.float8_e4m3fn, 7), "e5m2": (ml_dtypes.float8_e5m2, 14)}[fmt]
    v = np.moveaxis(np.asarray(x, np.float32).astype(ml_dtypes.bfloat16).astype(np.float64), axis, -1)
    blocks = v.reshape(v.shape[:-1] + (-1, 32))
    amax = np.abs(blocks).max(-1, keepdims=True)
    byte = np.maximum(np.where(amax > 0, np.frexp(amax)[1] - 1 + 127, 0) - down, 1)
    scale = np.exp2(byte - 127.0)
    codes = (blocks / scale).astype(np.float32).astype(dtype).astype(np.float64)
    return np.moveaxis((codes * scale).reshape(v.shape), -1, axis)


WIDE = False


def mx_kscale(k):
    if not WIDE:
        return np.ones(k)
    levels = np.array([10, -10, 5, -5, 0])
    if k % 512:
        return np.exp2(np.random.permutation(np.resize(levels, k // 32))).repeat(32)
    a = np.empty((k // 512, 16))
    for p in range(k // 512):
        a[p, :8] = np.random.permutation(np.resize(levels, 8))
        for g in range(8):
            far = levels[np.abs(levels - a[p, g]) >= 10]
            a[p, g + 8] = far[np.random.randint(len(far))]
    return np.exp2(a.ravel()).repeat(32)


def f64(x):
    return np.asarray(x).astype(np.float64)


def striped(idx):
    return np.tile(idx.reshape(-1, 16).T, (8, 1)).astype(np.uint16)


def unstriped(offs):
    return offs[:16].T.reshape(-1).astype(np.int64)


E2M1 = np.array([0.0, 0.5, 1.0, 1.5, 2.0, 3.0, 4.0, 6.0, -0.0, -0.5, -1.0, -1.5, -2.0, -3.0, -4.0, -6.0])


def pack_weight(w, fmt):
    k, n = w.shape
    w = f64(np.asarray(w, np.float32).astype(ml_dtypes.bfloat16)).reshape(k // 32, 32, n)
    amax = np.abs(w).max(1)
    if fmt == "e4m3":
        byte = np.frexp(amax)[1] - 1 + 127 - 7
    else:
        mant, ex = np.frexp(amax / 6.0)
        byte = np.where(mant > 0.5, ex, ex - 1) + 127
    byte = np.clip(np.where(amax > 0, byte, 1), 1, 254)
    scaled = (w * np.exp2(127.0 - byte)[:, None, :]).reshape(k, n).astype(np.float32)
    by_word = np.ascontiguousarray(scaled.reshape(k // 512, 128, 4, n).transpose(0, 1, 3, 2))
    if fmt == "e4m3":
        words = by_word.astype(ml_dtypes.float8_e4m3fn).view(np.uint8)
    else:
        c = by_word.astype(ml_dtypes.float4_e2m1fn).view(np.uint8) & 0xF
        words = (c[..., 0::2] | (c[..., 1::2] << 4)).reshape(k // 512, 128, 2 * n)
    return np.ascontiguousarray(words), np.ascontiguousarray(byte.astype(np.uint8).reshape(k // 512, 16, n))


def unpack_weight(words, scales, fmt):
    g, _, n = scales.shape
    words = np.ascontiguousarray(words).reshape(g, 128, n, -1)
    if fmt == "e4m3":
        vals = words.view(ml_dtypes.float8_e4m3fn).astype(np.float64)
    else:
        nib = np.empty((g, 128, n, 4), np.uint8)
        nib[..., 0::2] = words & 0xF
        nib[..., 1::2] = words >> 4
        vals = E2M1[nib]
    vals = vals * np.repeat(np.exp2(scales.astype(np.float64) - 127.0), 8, axis=1)[..., None]
    return vals.transpose(0, 1, 3, 2).reshape(g * 512, n)


def gelu(v):
    return 0.5 * v * (1.0 + np.tanh(np.sqrt(2.0 / np.pi) * (v + 0.044715 * v**3)))


K, T, E, C, H, N, HOT = 1024, 512, 4, 256, 512, 128, 2


def by_expert(wq, xq):
    return np.concatenate([wq[e].T @ xq[:, e * C:(e + 1) * C] for e in range(E)], axis=1)


def setup_inputs():
    n = np.random.standard_normal
    s = mx_kscale(K)
    u = mx_kscale(H)
    first = np.random.permutation(np.repeat(np.arange(E), T // E))
    second = (first + 1 + np.random.permutation(np.repeat(np.arange(E - 1), -(-T // (E - 1)))[:T])) % E
    while np.bincount(second, minlength=E).max() != T // E:
        load = np.bincount(second, minlength=E); hi, lo = int(load.argmax()), int(load.argmin())
        t = np.flatnonzero((second == hi) & (first != lo))[0]; second[t] = lo
    slot_token = np.empty(E * C, np.int64); pos = np.empty((2, T), np.int64); fill = np.zeros(E, np.int64)
    place = np.stack([np.random.permutation(C) for _ in range(E)])
    for r, deal in enumerate((first, second)):
        for t in np.random.permutation(T):
            e = deal[t]; j = e * C + place[e, fill[e]]; fill[e] += 1; slot_token[j] = t; pos[r, t] = j
    g = np.random.uniform(0.2, 0.8, T)
    x = pack_weight(n((K, T)) * s[:, None], "e4m3")
    w1h = [pack_weight(m, "e4m3") for m in n((HOT, K, H)) / np.sqrt(K) / s[None, :, None]]
    w3h = [pack_weight(m, "e4m3") for m in n((HOT, K, H)) / np.sqrt(K) / s[None, :, None] * u]
    w2h = [pack_weight(m, "e4m3") for m in n((HOT, H, N)) / np.sqrt(H) / u[None, :, None]]
    w1c = [pack_weight(m, "e2m1") for m in n((E - HOT, K, H)) / np.sqrt(K) / s[None, :, None]]
    w3c = [pack_weight(m, "e2m1") for m in n((E - HOT, K, H)) / np.sqrt(K) / s[None, :, None] * u]
    w2c = [pack_weight(m, "e2m1") for m in n((E - HOT, H, N)) / np.sqrt(H) / u[None, :, None]]
    return {
        "x_words": x[0],
        "x_scales": x[1],
        "w1h_words": np.stack([m[0] for m in w1h]),
        "w1h_scales": np.stack([m[1] for m in w1h]),
        "w3h_words": np.stack([m[0] for m in w3h]),
        "w3h_scales": np.stack([m[1] for m in w3h]),
        "w2h_words": np.stack([m[0] for m in w2h]),
        "w2h_scales": np.stack([m[1] for m in w2h]),
        "w1c_words": np.stack([m[0] for m in w1c]),
        "w1c_scales": np.stack([m[1] for m in w1c]),
        "w3c_words": np.stack([m[0] for m in w3c]),
        "w3c_scales": np.stack([m[1] for m in w3c]),
        "w2c_words": np.stack([m[0] for m in w2c]),
        "w2c_scales": np.stack([m[1] for m in w2c]),
        "gate": np.stack([np.tile(g, (128, 1)), np.tile(1.0 - g, (128, 1))]).astype(np.float32),
        "offs": striped(slot_token),
        "pos1": striped(pos[0]),
        "pos2": striped(pos[1]),
    }


def reference(x_words, x_scales, w1h_words, w1h_scales, w3h_words, w3h_scales, w2h_words, w2h_scales, w1c_words, w1c_scales, w3c_words, w3c_scales, w2c_words, w2c_scales, gate, offs, pos1, pos2):
    w1h = np.stack([unpack_weight(w1h_words[e], w1h_scales[e], "e4m3") for e in range(HOT)])
    w3h = np.stack([unpack_weight(w3h_words[e], w3h_scales[e], "e4m3") for e in range(HOT)])
    w2h = np.stack([unpack_weight(w2h_words[e], w2h_scales[e], "e4m3") for e in range(HOT)])
    w1c = np.stack([unpack_weight(w1c_words[e], w1c_scales[e], "e2m1") for e in range(E - HOT)])
    w3c = np.stack([unpack_weight(w3c_words[e], w3c_scales[e], "e2m1") for e in range(E - HOT)])
    w2c = np.stack([unpack_weight(w2c_words[e], w2c_scales[e], "e2m1") for e in range(E - HOT)])
    idx = unstriped(offs)
    xq = unpack_weight(x_words, x_scales, "e4m3")[:, idx]
    w1 = [*w1h, *w1c]
    w3 = [*w3h, *w3c]
    w2 = [*w2h, *w2c]
    h = gelu(by_expert(w1, xq)) * by_expert(w3, xq)
    y = by_expert(w2, mxq(h, 0, "e4m3"))
    out = sum(f64(gate[r, :1]) * y[:, unstriped(p)] for r, p in enumerate((pos1, pos2)))
    return out

@@ -1,0 +1,269 @@
+from contextlib import ExitStack
+
+import concourse.mybir as mybir
+from concourse.masks import make_identity
+
+K, T, E, C, H, N, HOT = 1024, 512, 4, 256, 512, 128, 2
+FLOPS = 2 * E * C * (2 * K * H + H * N)
+
+F32 = mybir.dt.float32
+BF16 = mybir.dt.bfloat16
+I32 = mybir.dt.int32
+U32 = mybir.dt.uint32
+U16 = mybir.dt.uint16
+U8 = mybir.dt.uint8
+FP8X4 = mybir.dt.float8_e4m3fn_x4
+FP4X4 = mybir.dt.float4_e2m1fn_x4
+MULT = mybir.AluOpType.mult
+ADD = mybir.AluOpType.add
+GELU = mybir.ActivationFunctionType.Gelu_apprx_tanh
+
+P = 128
+PASSES = 2
+COLD = E - HOT
+QUADS = 4
+AL = 64
+
+
+def tile_moe_hot_glu_gelu_kernel(
+    tc, x_words, x_scales, w1h_words, w1h_scales, w3h_words, w3h_scales, w2h_words, w2h_scales,
+    w1c_words, w1c_scales, w3c_words, w3c_scales, w2c_words, w2c_scales, gate, offs, pos1, pos2, out,
+):
+    nc = tc.nc
+    with ExitStack() as ctx:
+        lists = ctx.enter_context(tc.tile_pool(name="lists", bufs=1))
+        keep = ctx.enter_context(tc.tile_pool(name="keep", bufs=1))
+        work = ctx.enter_context(tc.tile_pool(name="work", bufs=3))
+        psum = ctx.enter_context(tc.psum_pool(name="psum", bufs=1))
+
+        offs_t = lists.tile([P, E * C // 16], U16, name="offs_t")
+        pos_t = [lists.tile([P, T // 16], U16, name=f"pos_t{r}") for r in range(2)]
+
+        xw = [keep.tile([P, T], I32, name=f"xw{s}", align_bytes=AL) for s in range(PASSES)]
+        xs_pair = keep.tile([P, 2, T], U8, align_bytes=AL)
+        xs_both, xs_last = xs_pair[:, 0, :], xs_pair[:, 1, :]
+        wh = [[keep.tile([P, PASSES, H], I32, name=f"wh{m}{e}", align_bytes=AL) for e in range(HOT)] for m in range(2)]
+        wc = [keep.tile([P, COLD * PASSES, 2 * H], U8, name=f"wc{m}", align_bytes=AL) for m in range(2)]
+        sh_pair = keep.tile([P, 2, H], U8, align_bytes=AL)
+        sh = [sh_pair[:, m, :] for m in range(2)]
+        sc_pair = keep.tile([P, 2, COLD * PASSES, H], U8, align_bytes=AL)
+        sc = [sc_pair[:, m] for m in range(2)]
+        w2h = keep.tile([P, HOT, N], I32, align_bytes=AL)
+        w2c = keep.tile([P, COLD, 2 * N], U8, align_bytes=AL)
+        s2 = keep.tile([P, 1 + COLD, N], U8, align_bytes=AL)
+        s2h, s2c = s2[:, 0, :], s2[:, 1:, :]
+        gate_t = keep.tile([P, 2, T], F32, align_bytes=AL)
+        ident = keep.tile([P, P], F32, align_bytes=AL)
+        y_all = keep.tile([P, E * C], F32, align_bytes=AL)
+        warm_out = keep.tile([P, 8], F32, align_bytes=AL)
+
+        nc.vector.memset(sh_pair[:].bitcast(I32), 0)
+        nc.vector.memset(xs_pair[:].bitcast(I32), 0)
+        nc.vector.memset(sc_pair[:].bitcast(I32), 0)
+        nc.vector.memset(s2[:].bitcast(I32), 0)
+
+        def quad_rows(q, n):
+            return slice(32 * q, 32 * q + n)
+
+        def blocks(q):
+            return slice(4 * q, 4 * q + 4)
+
+        def load_packed(eng, plane, scales, q):
+            src = scales.rearrange("e s b i -> (e s) b i")
+            eng.dma_start(plane[quad_rows(q, 4 * src.shape[0]), :].bitcast(I32), src[:, blocks(q), :].bitcast(I32))
+
+        def load_side(eng, plane, scales, q):
+            src = scales.rearrange("e s b i -> b (e s) i")
+            eng.dma_start(plane[quad_rows(q, 4), :, :].bitcast(I32), src[blocks(q), :, :].bitcast(I32))
+
+        def load_hot(eng, m, e):
+            src = (w1h_words, w3h_words)[m][e].rearrange("s p i d -> p s (i d)")
+            eng.dma_start(wh[m][e][:], src.bitcast(I32))
+
+        def load_cold(eng, m):
+            src = (w1c_words, w3c_words)[m].rearrange("f s p c -> p (f s) c")
+            eng.dma_start(wc[m][:].bitcast(I32), src.bitcast(I32))
+
+        load_packed(nc.scalar, sh[1], w3h_scales, 0)
+        load_packed(nc.sync, sh[0], w1h_scales, 3)
+        nc.sync.dma_start(xs_both[quad_rows(2, 8), :].bitcast(I32), x_scales[:, blocks(2), :].bitcast(I32))
+        load_packed(nc.scalar, sh[0], w1h_scales, 2)
+        nc.scalar.dma_start(xs_both[quad_rows(1, 8), :].bitcast(I32), x_scales[:, blocks(1), :].bitcast(I32))
+        nc.sync.dma_start(offs_t[:], offs)
+        nc.gpsimd.dma_start(xs_both[quad_rows(3, 8), :].bitcast(I32), x_scales[:, blocks(3), :].bitcast(I32))
+        nc.scalar.dma_start(xw[0][:], x_words[0].rearrange("p t d -> p (t d)").bitcast(I32))
+        nc.scalar.dma_start(xs_both[quad_rows(0, 8), :].bitcast(I32), x_scales[:, blocks(0), :].bitcast(I32))
+        load_packed(nc.scalar, sh[0], w1h_scales, 0)
+        load_hot(nc.sync, 0, 0)
+        load_packed(nc.sync, sh[1], w3h_scales, 2)
+        load_packed(nc.scalar, sh[1], w3h_scales, 1)
+        load_packed(nc.sync, sh[0], w1h_scales, 1)
+        load_hot(nc.sync, 1, 1)
+        nc.sync.dma_start(xw[1][:], x_words[1].rearrange("p t d -> p (t d)").bitcast(I32))
+        make_identity(nc, ident[:])
+        nc.scalar.activation(warm_out[:], ident[:, 0:8], GELU)
+        load_hot(nc.scalar, 0, 1)
+        load_side(nc.gpsimd, sc[0], w1c_scales, 3)
+        load_hot(nc.sync, 1, 0)
+        nc.scalar.dma_start(xs_last[quad_rows(3, 4), :].bitcast(I32), x_scales[1, blocks(3), :].bitcast(I32))
+        load_side(nc.gpsimd, sc[0], w1c_scales, 0)
+        load_packed(nc.gpsimd, sh[1], w3h_scales, 3)
+        load_side(nc.gpsimd, sc[1], w3c_scales, 0)
+        nc.gpsimd.dma_start(xs_last[quad_rows(0, 4), :].bitcast(I32), x_scales[1, blocks(0), :].bitcast(I32))
+        nc.scalar.dma_start(xs_last[quad_rows(2, 4), :].bitcast(I32), x_scales[1, blocks(2), :].bitcast(I32))
+        load_side(nc.gpsimd, sc[1], w3c_scales, 2)
+        nc.sync.dma_start(pos_t[1][:], pos2)
+        load_cold(nc.sync, 0)
+        load_cold(nc.sync, 1)
+        nc.scalar.dma_start(xs_last[quad_rows(1, 4), :].bitcast(I32), x_scales[1, blocks(1), :].bitcast(I32))
+        load_side(nc.gpsimd, sc[0], w1c_scales, 2)
+        load_side(nc.sync, sc[1], w3c_scales, 1)
+        load_side(nc.sync, s2c, w2c_scales, 0)
+        load_side(nc.scalar, sc[0], w1c_scales, 1)
+        load_side(nc.sync, s2c, w2c_scales, 2)
+        load_packed(nc.gpsimd, s2h, w2h_scales, 0)
+        nc.sync.dma_start(w2c[:].bitcast(I32), w2c_words.rearrange("f s p c -> p (f s) c").bitcast(I32))
+        load_packed(nc.sync, s2h, w2h_scales, 1)
+        load_side(nc.sync, sc[1], w3c_scales, 3)
+        load_side(nc.gpsimd, s2c, w2c_scales, 1)
+        load_side(nc.sync, s2c, w2c_scales, 3)
+        load_packed(nc.sync, s2h, w2h_scales, 2)
+        nc.sync.dma_start(gate_t[:], gate.rearrange("r p t -> p r t"))
+        load_packed(nc.sync, s2h, w2h_scales, 3)
+        nc.sync.dma_start(w2h[:], w2h_words.rearrange("e s p n d -> p (e s) (n d)").bitcast(I32))
+        nc.sync.dma_start(pos_t[0][:], pos1)
+
+        gw = {}
+        gs = {}
+
+        def picks(e):
+            return offs_t[:, e * C // 16 : (e + 1) * C // 16]
+
+        def gather_words(e, s):
+            gw[e, s] = keep.tile([P, C], U32, name=f"gw{e}{s}", tag=f"gw{s}", bufs=4, align_bytes=AL)
+            nc.vector.tensor_copy(gw[e, s][:], xw[s][:].bitcast(U32).indirect(picks(e)))
+
+        def gather_scales(e):
+            both = keep.tile([P, C], U8, name=f"gsb{e}", tag="gsb", bufs=4, align_bytes=AL)
+            nc.vector.tensor_copy(both[:], xs_both.indirect(picks(e)))
+            gs[e, 0] = both[:]
+            if e < HOT:
+                gs[e, 1] = both[4:P, :]
+
+        def gather_last(e):
+            last = keep.tile([P, C], U8, name=f"gsl{e}", align_bytes=AL)
+            nc.vector.tensor_copy(last[:], xs_last.indirect(picks(e)))
+            gs[e, 1] = last[:]
+
+        def first_layer(e, t, halves):
+            cols = slice(t * P, (t + 1) * P)
+            acc = []
+            for m in range(2):
+                bank = psum.tile([P, H], F32, name=f"acc{m}", tag=f"acc{m}", bufs=(2, 3)[m])
+                for s in range(PASSES):
+                    if e < HOT:
+                        rhs = wh[m][e][:, s, :].bitcast(FP8X4)
+                        rhs_scale = sh[m][4 * (PASSES * e + s) : P, :]
+                    else:
+                        rhs = wc[m][:, PASSES * (e - HOT) + s, :].bitcast(FP4X4)
+                        rhs_scale = sc[m][:, PASSES * (e - HOT) + s, :]
+                    nc.tensor.matmul_mx(
+                        out=bank[:], lhsT=gw[e, s][:, cols].bitcast(FP8X4), lhsT_scale=gs[e, s][:, cols],
+                        rhs=rhs, rhs_scale=rhs_scale, start=(s == 0), stop=(s == PASSES - 1),
+                    )
+                acc.append(bank)
+            act = work.tile([P, 2, P, 2], F32, name="act", align_bytes=AL)
+            nc.scalar.activation(act[:], acc[0][:].rearrange("j (p u v) -> j u p v", u=2, v=2), GELU)
+            h = work.tile([P, 2, P, 2], BF16, name="h", align_bytes=AL, bufs=8)
+            lin = acc[1][:].rearrange("j (p u v) -> j u p v", u=2, v=2)
+            if halves:
+                for u in range(2):
+                    nc.vector.tensor_tensor(h[:, u], lin[:, u], act[:, u], MULT)
+            else:
+                nc.vector.tensor_tensor(h[:], lin, act[:], MULT)
+            return h
+
+        def turn(hs):
+            bank = psum.tile([P, 2, 2, P], F32, name="turned", tag="late", bufs=3)
+            for t, h in enumerate(hs):
+                for u in range(2):
+                    nc.tensor.transpose(bank[:, t, u, :], h[:, u].rearrange("j p v -> j (p v)").bitcast(F32), ident[:])
+            n = len(hs)
+            ht = work.tile([P, 2 * P * 4], BF16, name="ht", align_bytes=AL, bufs=5)
+            nc.scalar.copy(
+                ht[:, 0 : n * P * 4].bitcast(F32).rearrange("p (t j u) -> p t j u", t=n, u=2),
+                bank[:, 0:n].rearrange("p t u j -> p t j u"),
+            )
+            hq = work.tile([P, C], U32, name="hq", align_bytes=AL, bufs=5)
+            hscale = work.tile([P, C], U8, name="hscale", align_bytes=AL, bufs=5)
+            nc.vector.quantize_mx(out=hq[:, 0 : n * P].bitcast(FP8X4), scales=hscale[:, 0 : n * P], in_=ht[:, 0 : n * P * 4])
+            return hq, hscale
+
+        def second_layer(e, slot0, n, hq, hscale):
+            bank = psum.tile([P, C], F32, name="ybank", tag="late", bufs=3)
+            if e < HOT:
+                lhsT, lhsT_scale = w2h[:, e, :].bitcast(FP8X4), s2h[4 * e : P, :]
+            else:
+                lhsT, lhsT_scale = w2c[:, e - HOT, :].bitcast(FP4X4), s2c[:, e - HOT, :]
+            nc.tensor.matmul_mx(
+                out=bank[:, 0:n], lhsT=lhsT, lhsT_scale=lhsT_scale,
+                rhs=hq[:, 0:n].bitcast(FP8X4), rhs_scale=hscale[:, 0:n], start=True, stop=True,
+            )
+            nc.scalar.copy(y_all[:, slot0 : slot0 + n], bank[:, 0:n])
+
+        gather_words(0, 0)
+        gather_scales(0)
+        gather_words(0, 1)
+        h01 = first_layer(0, 1, False)
+        gather_scales(1)
+        gather_last(2)
+        gather_words(1, 0)
+        gather_scales(2)
+        gather_words(1, 1)
+        h00 = first_layer(0, 0, False)
+        q0001 = turn([h00, h01])
+        gather_words(2, 0)
+        h11 = first_layer(1, 1, False)
+        h10 = first_layer(1, 0, False)
+        gather_words(2, 1)
+        h20 = first_layer(2, 0, False)
+        gather_scales(3)
+        gather_words(3, 1)
+        gather_words(3, 0)
+        gather_last(3)
+        q1011 = turn([h10, h11])
+        second_layer(1, 256, 256, *q1011)
+        h30 = first_layer(3, 0, False)
+        q30 = turn([h30])
+        second_layer(0, 0, 256, *q0001)
+        h21 = first_layer(2, 1, False)
+        h31 = first_layer(3, 1, True)
+        q2021 = turn([h20, h21])
+        second_layer(2, 512, 256, *q2021)
+        q31 = turn([h31])
+        second_layer(3, 768, 128, *q30)
+        second_layer(3, 896, 128, *q31)
+
+        half = T // 2
+        parts = {}
+        for c in range(2):
+            for r in range(2):
+                parts[c, r] = keep.tile([P, half], F32, name=f"part{c}{r}", align_bytes=AL)
+
+        def pick(c, r):
+            nc.vector.tensor_tensor(
+                parts[c, r][:], y_all[:].indirect(pos_t[r][:, c * half // 16 : (c + 1) * half // 16]),
+                gate_t[:, r, c * half : (c + 1) * half], MULT,
+            )
+
+        def finish(c):
+            total = keep.tile([P, half], F32, name=f"total{c}", align_bytes=AL)
+            nc.vector.tensor_tensor(total[:], parts[c, 0][:], parts[c, 1][:], ADD)
+            nc.sync.dma_start(out[:, c * half : (c + 1) * half], total[:])
+
+        pick(0, 0)
+        pick(0, 1)
+        pick(1, 0)
+        finish(0)
+        pick(1, 1)
+        finish(1)

@@ -40,9 +40,11 @@ def tile_moe_hot_glu_gelu_kernel(
         pos_t = [lists.tile([P, T // 16], U16, name=f"pos_t{r}") for r in range(2)]
 
         xw = [keep.tile([P, T], I32, name=f"xw{s}", align_bytes=AL) for s in range(PASSES)]
-        xs_pair = keep.tile([P, 2, T], U8, align_bytes=AL)
-        xs_both, xs_last = xs_pair[:, 0, :], xs_pair[:, 1, :]
-        wh = [[keep.tile([P, PASSES, H], I32, name=f"wh{m}{e}", align_bytes=AL) for e in range(HOT)] for m in range(2)]
+        xs_both = keep.tile([P, T], U8, align_bytes=AL)
+        xs_last = keep.tile([P, COLD * C], U8, align_bytes=AL)
+        gs_cold = keep.tile([P, COLD * C], U8, align_bytes=AL)
+        wh_pair = [keep.tile([P, HOT, PASSES, H], I32, name=f"wh{m}", align_bytes=AL) for m in range(2)]
+        wh = [[wh_pair[m][:, e] for e in range(HOT)] for m in range(2)]
         wc = [keep.tile([P, COLD * PASSES, 2 * H], U8, name=f"wc{m}", align_bytes=AL) for m in range(2)]
         sh_pair = keep.tile([P, 2, H], U8, align_bytes=AL)
         sh = [sh_pair[:, m, :] for m in range(2)]
@@ -55,12 +57,15 @@ def tile_moe_hot_glu_gelu_kernel(
         gate_t = keep.tile([P, 2, T], F32, align_bytes=AL)
         ident = keep.tile([P, P], F32, align_bytes=AL)
         y_all = keep.tile([P, E * C], F32, align_bytes=AL)
+        warm = keep.tile([P, 8], F32, align_bytes=AL)
         warm_out = keep.tile([P, 8], F32, align_bytes=AL)
 
-        nc.vector.memset(sh_pair[:].bitcast(I32), 0)
-        nc.vector.memset(xs_pair[:].bitcast(I32), 0)
+        nc.gpsimd.memset(xs_both[:].bitcast(I32), 0)
         nc.vector.memset(sc_pair[:].bitcast(I32), 0)
+        nc.gpsimd.memset(sh_pair[:].bitcast(I32), 0)
+        nc.vector.memset(warm[:], 0.0)
         nc.vector.memset(s2[:].bitcast(I32), 0)
+        nc.vector.memset(xs_last[:].bitcast(I32), 0)
 
         def quad_rows(q, n):
             return slice(32 * q, 32 * q + n)
@@ -84,186 +89,214 @@ def tile_moe_hot_glu_gelu_kernel(
             src = (w1c_words, w3c_words)[m].rearrange("f s p c -> p (f s) c")
             eng.dma_start(wc[m][:].bitcast(I32), src.bitcast(I32))
 
-        load_packed(nc.scalar, sh[1], w3h_scales, 0)
-        load_packed(nc.sync, sh[0], w1h_scales, 3)
-        nc.sync.dma_start(xs_both[quad_rows(2, 8), :].bitcast(I32), x_scales[:, blocks(2), :].bitcast(I32))
-        load_packed(nc.scalar, sh[0], w1h_scales, 2)
-        nc.scalar.dma_start(xs_both[quad_rows(1, 8), :].bitcast(I32), x_scales[:, blocks(1), :].bitcast(I32))
-        nc.sync.dma_start(offs_t[:], offs)
-        nc.gpsimd.dma_start(xs_both[quad_rows(3, 8), :].bitcast(I32), x_scales[:, blocks(3), :].bitcast(I32))
-        nc.scalar.dma_start(xw[0][:], x_words[0].rearrange("p t d -> p (t d)").bitcast(I32))
-        nc.scalar.dma_start(xs_both[quad_rows(0, 8), :].bitcast(I32), x_scales[:, blocks(0), :].bitcast(I32))
-        load_packed(nc.scalar, sh[0], w1h_scales, 0)
-        load_hot(nc.sync, 0, 0)
-        load_packed(nc.sync, sh[1], w3h_scales, 2)
-        load_packed(nc.scalar, sh[1], w3h_scales, 1)
-        load_packed(nc.sync, sh[0], w1h_scales, 1)
-        load_hot(nc.sync, 1, 1)
-        nc.sync.dma_start(xw[1][:], x_words[1].rearrange("p t d -> p (t d)").bitcast(I32))
-        make_identity(nc, ident[:])
-        nc.scalar.activation(warm_out[:], ident[:, 0:8], GELU)
-        load_hot(nc.scalar, 0, 1)
-        load_side(nc.gpsimd, sc[0], w1c_scales, 3)
-        load_hot(nc.sync, 1, 0)
-        nc.scalar.dma_start(xs_last[quad_rows(3, 4), :].bitcast(I32), x_scales[1, blocks(3), :].bitcast(I32))
-        load_side(nc.gpsimd, sc[0], w1c_scales, 0)
-        load_packed(nc.gpsimd, sh[1], w3h_scales, 3)
-        load_side(nc.gpsimd, sc[1], w3c_scales, 0)
-        nc.gpsimd.dma_start(xs_last[quad_rows(0, 4), :].bitcast(I32), x_scales[1, blocks(0), :].bitcast(I32))
-        nc.scalar.dma_start(xs_last[quad_rows(2, 4), :].bitcast(I32), x_scales[1, blocks(2), :].bitcast(I32))
-        load_side(nc.gpsimd, sc[1], w3c_scales, 2)
-        nc.sync.dma_start(pos_t[1][:], pos2)
-        load_cold(nc.sync, 0)
-        load_cold(nc.sync, 1)
-        nc.scalar.dma_start(xs_last[quad_rows(1, 4), :].bitcast(I32), x_scales[1, blocks(1), :].bitcast(I32))
-        load_side(nc.gpsimd, sc[0], w1c_scales, 2)
-        load_side(nc.sync, sc[1], w3c_scales, 1)
-        load_side(nc.sync, s2c, w2c_scales, 0)
-        load_side(nc.scalar, sc[0], w1c_scales, 1)
-        load_side(nc.sync, s2c, w2c_scales, 2)
-        load_packed(nc.gpsimd, s2h, w2h_scales, 0)
-        nc.sync.dma_start(w2c[:].bitcast(I32), w2c_words.rearrange("f s p c -> p (f s) c").bitcast(I32))
-        load_packed(nc.sync, s2h, w2h_scales, 1)
-        load_side(nc.sync, sc[1], w3c_scales, 3)
-        load_side(nc.gpsimd, s2c, w2c_scales, 1)
-        load_side(nc.sync, s2c, w2c_scales, 3)
-        load_packed(nc.sync, s2h, w2h_scales, 2)
-        nc.sync.dma_start(gate_t[:], gate.rearrange("r p t -> p r t"))
-        load_packed(nc.sync, s2h, w2h_scales, 3)
-        nc.sync.dma_start(w2h[:], w2h_words.rearrange("e s p n d -> p (e s) (n d)").bitcast(I32))
-        nc.sync.dma_start(pos_t[0][:], pos1)
+        def load_cold_one(eng, m, f):
+            src = (w1c_words, w3c_words)[m][f].rearrange("s p c -> p s c")
+            eng.dma_start(wc[m][:, PASSES * f : PASSES * (f + 1), :].bitcast(I32), src.bitcast(I32))
 
-        gw = {}
-        gs = {}
+        def load_hot_pass(eng, m, s):
+            src = (w1h_words, w3h_words)[m][:, s].rearrange("e p i d -> p e (i d)")
+            eng.dma_start(wh_pair[m][:, :, s, :], src.bitcast(I32))
+
+        banks = [psum.tile([P, H], F32, name=f"bank{b}") for b in range(8)]
+        bank_of = {"a20":0,"a21":1,"a30":2,"a31":3,"T00":1,"T10":2,"b20":4,"b21":5,"b30":6,"b31":7,"T20":0,"T30":3,"T31":1,"y00":2,"y10":4,"y20":5,"y30":6,"y31":0,"a00":0,"a01":1,"a10":2,"a11":3,"b00":4,"b01":5,"b10":6,"b11":7}
+        tile_of = {"W00":"W00","W01":"W01","S0":"S0","W10":"W10","W11":"W11","S1":"S1","W20":"W20","W21":"W21","S2":"S2","W30":"W30","W31":"W31","S3":"S3"}
+        gathered = {}
+        for name in sorted(set(tile_of.values())):
+            gathered[name] = keep.tile([P, C], U32 if name.startswith("W") else U8, name=f"g{name}", align_bytes=AL)
+        on_vector = []
+
+        def evacuate(key, dst, src):
+            if key in on_vector:
+                nc.vector.tensor_copy(dst, src)
+            else:
+                nc.scalar.copy(dst, src)
+
+        gw, gs, act, h, hq, hscale = {}, {}, {}, {}, {}, {}
 
         def picks(e):
             return offs_t[:, e * C // 16 : (e + 1) * C // 16]
 
         def gather_words(e, s):
-            gw[e, s] = keep.tile([P, C], U32, name=f"gw{e}{s}", tag=f"gw{s}", bufs=4, align_bytes=AL)
+            gw[e, s] = gathered[tile_of[f"W{e}{s}"]]
             nc.vector.tensor_copy(gw[e, s][:], xw[s][:].bitcast(U32).indirect(picks(e)))
 
         def gather_scales(e):
-            both = keep.tile([P, C], U8, name=f"gsb{e}", tag="gsb", bufs=4, align_bytes=AL)
-            nc.vector.tensor_copy(both[:], xs_both.indirect(picks(e)))
-            gs[e, 0] = both[:]
             if e < HOT:
+                both = gathered[tile_of[f"S{e}"]][:]
                 gs[e, 1] = both[4:P, :]
+            else:
+                both = gs_cold[:, (e - HOT) * C : (e - HOT + 1) * C]
+                gs[e, 1] = xs_last[:, (e - HOT) * C : (e - HOT + 1) * C]
+            nc.vector.tensor_copy(both, xs_both[:].indirect(picks(e)))
+            gs[e, 0] = both
 
-        def gather_last(e):
-            last = keep.tile([P, C], U8, name=f"gsl{e}", align_bytes=AL)
-            nc.vector.tensor_copy(last[:], xs_last.indirect(picks(e)))
-            gs[e, 1] = last[:]
+        def move_last_pass_scales(eng, q):
+            eng.dma_start(xs_last[quad_rows(q, 4), :].bitcast(I32), gs_cold[32 * q + 4 : 32 * q + 8, :].bitcast(I32))
 
-        def first_layer(e, t, halves):
+        def first_layer(m, e, t):
             cols = slice(t * P, (t + 1) * P)
-            acc = []
-            for m in range(2):
-                bank = psum.tile([P, H], F32, name=f"acc{m}", tag=f"acc{m}", bufs=(2, 3)[m])
-                for s in range(PASSES):
-                    if e < HOT:
-                        rhs = wh[m][e][:, s, :].bitcast(FP8X4)
-                        rhs_scale = sh[m][4 * (PASSES * e + s) : P, :]
-                    else:
-                        rhs = wc[m][:, PASSES * (e - HOT) + s, :].bitcast(FP4X4)
-                        rhs_scale = sc[m][:, PASSES * (e - HOT) + s, :]
-                    nc.tensor.matmul_mx(
-                        out=bank[:], lhsT=gw[e, s][:, cols].bitcast(FP8X4), lhsT_scale=gs[e, s][:, cols],
-                        rhs=rhs, rhs_scale=rhs_scale, start=(s == 0), stop=(s == PASSES - 1),
-                    )
-                acc.append(bank)
-            act = work.tile([P, 2, P, 2], F32, name="act", align_bytes=AL)
-            nc.scalar.activation(act[:], acc[0][:].rearrange("j (p u v) -> j u p v", u=2, v=2), GELU)
-            h = work.tile([P, 2, P, 2], BF16, name="h", align_bytes=AL, bufs=8)
-            lin = acc[1][:].rearrange("j (p u v) -> j u p v", u=2, v=2)
+            bank = banks[bank_of["ab"[m] + f"{e}{t}"]]
+            for s in range(PASSES):
+                if e < HOT:
+                    rhs = wh[m][e][:, s, :].bitcast(FP8X4)
+                    rhs_scale = sh[m][4 * (PASSES * e + s) : P, :]
+                else:
+                    rhs = wc[m][:, PASSES * (e - HOT) + s, :].bitcast(FP4X4)
+                    rhs_scale = sc[m][:, PASSES * (e - HOT) + s, :]
+                nc.tensor.matmul_mx(
+                    out=bank[:], lhsT=gw[e, s][:, cols].bitcast(FP8X4), lhsT_scale=gs[e, s][:, cols],
+                    rhs=rhs, rhs_scale=rhs_scale, start=(s == 0), stop=(s == PASSES - 1),
+                )
+            return bank[:].rearrange("j (p u v) -> j u p v", u=2, v=2)
+
+        def gate_half(e, t):
+            act[e, t] = work.tile([P, 2, P, 2], F32, name="act", align_bytes=AL, bufs=8)
+            nc.scalar.activation(act[e, t][:], first_layer(0, e, t), GELU)
+
+        def linear_half(e, t, halves):
+            lin = first_layer(1, e, t)
+            h[e, t] = work.tile([P, 2, P, 2], BF16, name="h", align_bytes=AL, bufs=8)
             if halves:
                 for u in range(2):
-                    nc.vector.tensor_tensor(h[:, u], lin[:, u], act[:, u], MULT)
+                    nc.vector.tensor_tensor(h[e, t][:, u], lin[:, u], act[e, t][:, u], MULT)
             else:
-                nc.vector.tensor_tensor(h[:], lin, act[:], MULT)
-            return h
+                nc.vector.tensor_tensor(h[e, t][:], lin, act[e, t][:], MULT)
 
-        def turn(hs):
-            bank = psum.tile([P, 2, 2, P], F32, name="turned", tag="late", bufs=3)
-            for t, h in enumerate(hs):
+        def linear_half_pool(e, t):
+            lin = work.tile([P, 2, P, 2], F32, name="lin", align_bytes=AL, bufs=4)
+            nc.scalar.copy(lin[:], first_layer(1, e, t))
+            h[e, t] = work.tile([P, 2, P, 2], BF16, name="h", align_bytes=AL, bufs=8)
+            flat = "j u p v -> j (u p v)"
+            nc.gpsimd.tensor_tensor(h[e, t][:].rearrange(flat), lin[:].rearrange(flat), act[e, t][:].rearrange(flat), MULT)
+
+        def turn(e, t0, n):
+            bank = banks[bank_of[f"T{e}{t0}"]][:].rearrange("p (t u j) -> p t u j", t=2, u=2)
+            for t in range(n):
                 for u in range(2):
-                    nc.tensor.transpose(bank[:, t, u, :], h[:, u].rearrange("j p v -> j (p v)").bitcast(F32), ident[:])
-            n = len(hs)
-            ht = work.tile([P, 2 * P * 4], BF16, name="ht", align_bytes=AL, bufs=5)
-            nc.scalar.copy(
-                ht[:, 0 : n * P * 4].bitcast(F32).rearrange("p (t j u) -> p t j u", t=n, u=2),
+                    words = h[e, t0 + t][:, u].rearrange("j p v -> j (p v)").bitcast(F32)
+                    nc.tensor.transpose(bank[:, t, u, :], words, ident[:])
+            ht = work.tile([P, n * P * 4], BF16, name="ht", align_bytes=AL, bufs=5)
+            evacuate(
+                f"ct{e}{t0}",
+                ht[:].bitcast(F32).rearrange("p (t j u) -> p t j u", t=n, u=2),
                 bank[:, 0:n].rearrange("p t u j -> p t j u"),
             )
-            hq = work.tile([P, C], U32, name="hq", align_bytes=AL, bufs=5)
-            hscale = work.tile([P, C], U8, name="hscale", align_bytes=AL, bufs=5)
-            nc.vector.quantize_mx(out=hq[:, 0 : n * P].bitcast(FP8X4), scales=hscale[:, 0 : n * P], in_=ht[:, 0 : n * P * 4])
-            return hq, hscale
+            hq[e, t0] = work.tile([P, n * P], U32, name="hq", align_bytes=AL, bufs=5)
+            hscale[e, t0] = work.tile([P, n * P], U8, name="hscale", align_bytes=AL, bufs=5)
+            nc.vector.quantize_mx(out=hq[e, t0][:].bitcast(FP8X4), scales=hscale[e, t0][:], in_=ht[:])
 
-        def second_layer(e, slot0, n, hq, hscale):
-            bank = psum.tile([P, C], F32, name="ybank", tag="late", bufs=3)
+        def second_layer(e, t0, n):
+            bank = banks[bank_of[f"y{e}{t0}"]][:, 0 : n * P]
             if e < HOT:
                 lhsT, lhsT_scale = w2h[:, e, :].bitcast(FP8X4), s2h[4 * e : P, :]
             else:
                 lhsT, lhsT_scale = w2c[:, e - HOT, :].bitcast(FP4X4), s2c[:, e - HOT, :]
             nc.tensor.matmul_mx(
-                out=bank[:, 0:n], lhsT=lhsT, lhsT_scale=lhsT_scale,
-                rhs=hq[:, 0:n].bitcast(FP8X4), rhs_scale=hscale[:, 0:n], start=True, stop=True,
+                out=bank, lhsT=lhsT, lhsT_scale=lhsT_scale,
+                rhs=hq[e, t0][:].bitcast(FP8X4), rhs_scale=hscale[e, t0][:], start=True, stop=True,
             )
-            nc.scalar.copy(y_all[:, slot0 : slot0 + n], bank[:, 0:n])
+            slot0 = e * C + t0 * P
+            evacuate(f"cy{e}{t0}", y_all[:, slot0 : slot0 + n * P], bank)
 
+        make_identity(nc, ident[:])
+        nc.scalar.activation(warm_out[:], warm[:], GELU)
+        nc.sync.dma_start(xw[0][:], x_words[0].rearrange("p t d -> p (t d)").bitcast(I32))
+        nc.sync.dma_start(xs_both[quad_rows(0, 8), :].bitcast(I32), x_scales[:, blocks(0), :].bitcast(I32))
+        nc.sync.dma_start(xs_both[quad_rows(1, 8), :].bitcast(I32), x_scales[:, blocks(1), :].bitcast(I32))
+        nc.sync.dma_start(xs_both[quad_rows(2, 8), :].bitcast(I32), x_scales[:, blocks(2), :].bitcast(I32))
+        nc.sync.dma_start(xs_both[quad_rows(3, 8), :].bitcast(I32), x_scales[:, blocks(3), :].bitcast(I32))
+        nc.sync.dma_start(offs_t[:], offs)
+        nc.sync.dma_start(xw[1][:], x_words[1].rearrange("p t d -> p (t d)").bitcast(I32))
         gather_words(0, 0)
         gather_scales(0)
-        gather_words(0, 1)
-        h01 = first_layer(0, 1, False)
-        gather_scales(1)
-        gather_last(2)
         gather_words(1, 0)
-        gather_scales(2)
+        gather_scales(1)
+        gather_words(0, 1)
         gather_words(1, 1)
-        h00 = first_layer(0, 0, False)
-        q0001 = turn([h00, h01])
-        gather_words(2, 0)
-        h11 = first_layer(1, 1, False)
-        h10 = first_layer(1, 0, False)
-        gather_words(2, 1)
-        h20 = first_layer(2, 0, False)
+        gather_scales(2)
         gather_scales(3)
-        gather_words(3, 1)
+        gather_words(2, 0)
+        gather_words(2, 1)
         gather_words(3, 0)
-        gather_last(3)
-        q1011 = turn([h10, h11])
-        second_layer(1, 256, 256, *q1011)
-        h30 = first_layer(3, 0, False)
-        q30 = turn([h30])
-        second_layer(0, 0, 256, *q0001)
-        h21 = first_layer(2, 1, False)
-        h31 = first_layer(3, 1, True)
-        q2021 = turn([h20, h21])
-        second_layer(2, 512, 256, *q2021)
-        q31 = turn([h31])
-        second_layer(3, 768, 128, *q30)
-        second_layer(3, 896, 128, *q31)
+        gather_words(3, 1)
+        load_side(nc.gpsimd, sc[1], w3c_scales, 0)
+        load_side(nc.gpsimd, sc[1], w3c_scales, 1)
+        load_side(nc.gpsimd, sc[1], w3c_scales, 2)
+        load_side(nc.gpsimd, sc[1], w3c_scales, 3)
+        load_hot_pass(nc.sync, 0, 0)
+        load_packed(nc.sync, sh[0], w1h_scales, 0)
+        load_packed(nc.sync, sh[0], w1h_scales, 1)
+        load_packed(nc.sync, sh[0], w1h_scales, 2)
+        load_packed(nc.sync, sh[0], w1h_scales, 3)
+        load_hot_pass(nc.sync, 0, 1)
+        load_packed(nc.sync, sh[1], w3h_scales, 0)
+        load_packed(nc.sync, sh[1], w3h_scales, 1)
+        load_hot(nc.sync, 1, 0)
+        load_packed(nc.sync, sh[1], w3h_scales, 2)
+        load_packed(nc.sync, sh[1], w3h_scales, 3)
+        load_hot(nc.sync, 1, 1)
+        load_side(nc.sync, sc[0], w1c_scales, 0)
+        load_side(nc.sync, sc[0], w1c_scales, 1)
+        load_side(nc.sync, sc[0], w1c_scales, 2)
+        load_side(nc.sync, sc[0], w1c_scales, 3)
+        load_cold(nc.sync, 0)
+        load_cold(nc.sync, 1)
+        move_last_pass_scales(nc.sync, 0)
+        move_last_pass_scales(nc.sync, 1)
+        move_last_pass_scales(nc.sync, 2)
+        move_last_pass_scales(nc.sync, 3)
+        nc.sync.dma_start(w2h[:], w2h_words.rearrange("e s p n d -> p (e s) (n d)").bitcast(I32))
+        load_packed(nc.sync, s2h, w2h_scales, 0)
+        load_packed(nc.sync, s2h, w2h_scales, 1)
+        load_packed(nc.sync, s2h, w2h_scales, 2)
+        load_packed(nc.sync, s2h, w2h_scales, 3)
+        nc.sync.dma_start(w2c[:].bitcast(I32), w2c_words.rearrange("f s p c -> p (f s) c").bitcast(I32))
+        load_side(nc.sync, s2c, w2c_scales, 0)
+        load_side(nc.sync, s2c, w2c_scales, 1)
+        load_side(nc.sync, s2c, w2c_scales, 2)
+        load_side(nc.sync, s2c, w2c_scales, 3)
+        nc.sync.dma_start(pos_t[0][:], pos1)
+        nc.sync.dma_start(gate_t[:], gate.rearrange("r p t -> p r t"))
+        nc.sync.dma_start(pos_t[1][:], pos2)
+        gate_half(0, 0)
+        gate_half(0, 1)
+        gate_half(1, 0)
+        gate_half(1, 1)
+        linear_half(0, 0, False)
+        linear_half(0, 1, False)
+        linear_half(1, 0, False)
+        linear_half(1, 1, False)
+        gate_half(2, 0)
+        gate_half(2, 1)
+        gate_half(3, 0)
+        gate_half(3, 1)
+        turn(0, 0, 2)
+        turn(1, 0, 2)
+        linear_half(2, 0, False)
+        linear_half(2, 1, False)
+        linear_half(3, 0, False)
+        linear_half(3, 1, True)
+        turn(2, 0, 2)
+        turn(3, 0, 1)
+        turn(3, 1, 1)
+        second_layer(0, 0, 2)
+        second_layer(1, 0, 2)
+        second_layer(2, 0, 2)
+        second_layer(3, 0, 1)
+        second_layer(3, 1, 1)
 
         half = T // 2
-        parts = {}
+        first_part = keep.tile([P, T], F32, align_bytes=AL)
+        nc.vector.tensor_tensor(first_part[:], y_all[:].indirect(pos_t[0][:]), gate_t[:, 0, :], MULT)
+        second_part = keep.tile([P, T], F32, align_bytes=AL)
+        total = keep.tile([P, T], F32, align_bytes=AL)
         for c in range(2):
-            for r in range(2):
-                parts[c, r] = keep.tile([P, half], F32, name=f"part{c}{r}", align_bytes=AL)
-
-        def pick(c, r):
+            cols = slice(c * half, (c + 1) * half)
             nc.vector.tensor_tensor(
-                parts[c, r][:], y_all[:].indirect(pos_t[r][:, c * half // 16 : (c + 1) * half // 16]),
-                gate_t[:, r, c * half : (c + 1) * half], MULT,
+                second_part[:, cols], y_all[:].indirect(pos_t[1][:, c * half // 16 : (c + 1) * half // 16]),
+                gate_t[:, 1, cols], MULT,
             )
-
-        def finish(c):
-            total = keep.tile([P, half], F32, name=f"total{c}", align_bytes=AL)
-            nc.vector.tensor_tensor(total[:], parts[c, 0][:], parts[c, 1][:], ADD)
-            nc.sync.dma_start(out[:, c * half : (c + 1) * half], total[:])
-
-        pick(0, 0)
-        pick(0, 1)
-        pick(1, 0)
-        finish(0)
-        pick(1, 1)
-        finish(1)
+        for c in range(2):
+            cols = slice(c * half, (c + 1) * half)
+            nc.vector.tensor_tensor(total[:, cols], first_part[:, cols], second_part[:, cols], ADD)
+            nc.sync.dma_start(out[:, cols], total[:, cols])

@@ -41,8 +41,7 @@ def tile_moe_hot_glu_gelu_kernel(
 
         xw = [keep.tile([P, T], I32, name=f"xw{s}", align_bytes=AL) for s in range(PASSES)]
         xs_both = keep.tile([P, T], U8, align_bytes=AL)
-        xs_last = keep.tile([P, COLD * C], U8, align_bytes=AL)
-        gs_cold = keep.tile([P, COLD * C], U8, align_bytes=AL)
+        xs_last = keep.tile([P, T], U8, align_bytes=AL)
         wh_pair = [keep.tile([P, HOT, PASSES, H], I32, name=f"wh{m}", align_bytes=AL) for m in range(2)]
         wh = [[wh_pair[m][:, e] for e in range(HOT)] for m in range(2)]
         wc = [keep.tile([P, COLD * PASSES, 2 * H], U8, name=f"wc{m}", align_bytes=AL) for m in range(2)]
@@ -61,11 +60,11 @@ def tile_moe_hot_glu_gelu_kernel(
         warm_out = keep.tile([P, 8], F32, align_bytes=AL)
 
         nc.gpsimd.memset(xs_both[:].bitcast(I32), 0)
-        nc.vector.memset(sc_pair[:].bitcast(I32), 0)
         nc.gpsimd.memset(sh_pair[:].bitcast(I32), 0)
         nc.vector.memset(warm[:], 0.0)
-        nc.vector.memset(s2[:].bitcast(I32), 0)
         nc.vector.memset(xs_last[:].bitcast(I32), 0)
+        nc.vector.memset(sc_pair[:].bitcast(I32), 0)
+        nc.vector.memset(s2[:].bitcast(I32), 0)
 
         def quad_rows(q, n):
             return slice(32 * q, 32 * q + n)
@@ -77,9 +76,9 @@ def tile_moe_hot_glu_gelu_kernel(
             src = scales.rearrange("e s b i -> (e s) b i")
             eng.dma_start(plane[quad_rows(q, 4 * src.shape[0]), :].bitcast(I32), src[:, blocks(q), :].bitcast(I32))
 
-        def load_side(eng, plane, scales, q):
-            src = scales.rearrange("e s b i -> b (e s) i")
-            eng.dma_start(plane[quad_rows(q, 4), :, :].bitcast(I32), src[blocks(q), :, :].bitcast(I32))
+        def load_side(eng, plane, scales, r):
+            src = scales.rearrange("e s (q r) i -> r q (e s) i", r=4)
+            eng.dma_start(plane[r:P:32, :, :].bitcast(I32), src[r].bitcast(I32))
 
         def load_hot(eng, m, e):
             src = (w1h_words, w3h_words)[m][e].rearrange("s p i d -> p s (i d)")
@@ -98,8 +97,8 @@ def tile_moe_hot_glu_gelu_kernel(
             eng.dma_start(wh_pair[m][:, :, s, :], src.bitcast(I32))
 
         banks = [psum.tile([P, H], F32, name=f"bank{b}") for b in range(8)]
-        bank_of = {"a20":0,"a21":1,"a30":2,"a31":3,"T00":1,"T10":2,"b20":4,"b21":5,"b30":6,"b31":7,"T20":0,"T30":3,"T31":1,"y00":2,"y10":4,"y20":5,"y30":6,"y31":0,"a00":0,"a01":1,"a10":2,"a11":3,"b00":4,"b01":5,"b10":6,"b11":7}
-        tile_of = {"W00":"W00","W01":"W01","S0":"S0","W10":"W10","W11":"W11","S1":"S1","W20":"W20","W21":"W21","S2":"S2","W30":"W30","W31":"W31","S3":"S3"}
+        bank_of = {"a00":0,"a01":1,"a10":2,"a11":3,"b00":4,"b01":5,"b10":6,"b11":7,"T00":3,"a20":0,"a21":1,"b20":2,"b21":4,"a30":5,"a31":3,"T10":5,"b30":6,"b31":7,"T20":0,"T30":1,"T31":3,"y00":2,"y10":4,"y20":5,"y30":6,"y31":0}
+        tile_of = {"W00":"W00","W01":"W01","S0":"S0","W10":"W10","W11":"W11","S1":"S1","W20":"W20","W21":"W21","S2":"S2","W30":"W30","W31":"W01","S3":"S3"}
         gathered = {}
         for name in sorted(set(tile_of.values())):
             gathered[name] = keep.tile([P, C], U32 if name.startswith("W") else U8, name=f"g{name}", align_bytes=AL)
@@ -121,17 +120,16 @@ def tile_moe_hot_glu_gelu_kernel(
             nc.vector.tensor_copy(gw[e, s][:], xw[s][:].bitcast(U32).indirect(picks(e)))
 
         def gather_scales(e):
+            both = gathered[tile_of[f"S{e}"]]
+            nc.vector.tensor_copy(both[:], xs_both[:].indirect(picks(e)))
+            gs[e, 0] = both[:]
             if e < HOT:
-                both = gathered[tile_of[f"S{e}"]][:]
                 gs[e, 1] = both[4:P, :]
-            else:
-                both = gs_cold[:, (e - HOT) * C : (e - HOT + 1) * C]
-                gs[e, 1] = xs_last[:, (e - HOT) * C : (e - HOT + 1) * C]
-            nc.vector.tensor_copy(both, xs_both[:].indirect(picks(e)))
-            gs[e, 0] = both
 
-        def move_last_pass_scales(eng, q):
-            eng.dma_start(xs_last[quad_rows(q, 4), :].bitcast(I32), gs_cold[32 * q + 4 : 32 * q + 8, :].bitcast(I32))
+        def gather_last(e):
+            last = gathered[{"B2":"S0","B3":"S1"}[f"B{e}"]]
+            nc.vector.tensor_copy(last[:], xs_last[:].indirect(picks(e)))
+            gs[e, 1] = last[:]
 
         def first_layer(m, e, t):
             cols = slice(t * P, (t + 1) * P)
@@ -207,44 +205,34 @@ def tile_moe_hot_glu_gelu_kernel(
         nc.sync.dma_start(xs_both[quad_rows(3, 8), :].bitcast(I32), x_scales[:, blocks(3), :].bitcast(I32))
         nc.sync.dma_start(offs_t[:], offs)
         nc.sync.dma_start(xw[1][:], x_words[1].rearrange("p t d -> p (t d)").bitcast(I32))
-        gather_words(0, 0)
-        gather_scales(0)
-        gather_words(1, 0)
-        gather_scales(1)
-        gather_words(0, 1)
-        gather_words(1, 1)
-        gather_scales(2)
-        gather_scales(3)
-        gather_words(2, 0)
-        gather_words(2, 1)
-        gather_words(3, 0)
-        gather_words(3, 1)
-        load_side(nc.gpsimd, sc[1], w3c_scales, 0)
-        load_side(nc.gpsimd, sc[1], w3c_scales, 1)
-        load_side(nc.gpsimd, sc[1], w3c_scales, 2)
-        load_side(nc.gpsimd, sc[1], w3c_scales, 3)
         load_hot_pass(nc.sync, 0, 0)
         load_packed(nc.sync, sh[0], w1h_scales, 0)
         load_packed(nc.sync, sh[0], w1h_scales, 1)
         load_packed(nc.sync, sh[0], w1h_scales, 2)
         load_packed(nc.sync, sh[0], w1h_scales, 3)
         load_hot_pass(nc.sync, 0, 1)
+        load_hot(nc.sync, 1, 0)
         load_packed(nc.sync, sh[1], w3h_scales, 0)
         load_packed(nc.sync, sh[1], w3h_scales, 1)
-        load_hot(nc.sync, 1, 0)
         load_packed(nc.sync, sh[1], w3h_scales, 2)
         load_packed(nc.sync, sh[1], w3h_scales, 3)
         load_hot(nc.sync, 1, 1)
+        nc.gpsimd.dma_start(xs_last[quad_rows(0, 4), :].bitcast(I32), x_scales[1, blocks(0), :].bitcast(I32))
+        nc.gpsimd.dma_start(xs_last[quad_rows(1, 4), :].bitcast(I32), x_scales[1, blocks(1), :].bitcast(I32))
+        nc.gpsimd.dma_start(xs_last[quad_rows(2, 4), :].bitcast(I32), x_scales[1, blocks(2), :].bitcast(I32))
+        nc.gpsimd.dma_start(xs_last[quad_rows(3, 4), :].bitcast(I32), x_scales[1, blocks(3), :].bitcast(I32))
         load_side(nc.sync, sc[0], w1c_scales, 0)
         load_side(nc.sync, sc[0], w1c_scales, 1)
         load_side(nc.sync, sc[0], w1c_scales, 2)
         load_side(nc.sync, sc[0], w1c_scales, 3)
-        load_cold(nc.sync, 0)
-        load_cold(nc.sync, 1)
-        move_last_pass_scales(nc.sync, 0)
-        move_last_pass_scales(nc.sync, 1)
-        move_last_pass_scales(nc.sync, 2)
-        move_last_pass_scales(nc.sync, 3)
+        load_cold_one(nc.sync, 0, 0)
+        load_cold_one(nc.sync, 1, 0)
+        load_side(nc.sync, sc[1], w3c_scales, 0)
+        load_side(nc.sync, sc[1], w3c_scales, 1)
+        load_side(nc.sync, sc[1], w3c_scales, 2)
+        load_side(nc.sync, sc[1], w3c_scales, 3)
+        load_cold_one(nc.sync, 0, 1)
+        load_cold_one(nc.sync, 1, 1)
         nc.sync.dma_start(w2h[:], w2h_words.rearrange("e s p n d -> p (e s) (n d)").bitcast(I32))
         load_packed(nc.sync, s2h, w2h_scales, 0)
         load_packed(nc.sync, s2h, w2h_scales, 1)
@@ -258,24 +246,38 @@ def tile_moe_hot_glu_gelu_kernel(
         nc.sync.dma_start(pos_t[0][:], pos1)
         nc.sync.dma_start(gate_t[:], gate.rearrange("r p t -> p r t"))
         nc.sync.dma_start(pos_t[1][:], pos2)
+        gather_words(0, 0)
+        gather_scales(0)
+        gather_words(1, 0)
+        gather_scales(1)
+        gather_words(0, 1)
+        gather_words(1, 1)
+        gather_words(2, 0)
+        gather_scales(2)
+        gather_words(2, 1)
+        gather_words(3, 0)
+        gather_scales(3)
         gate_half(0, 0)
         gate_half(0, 1)
         gate_half(1, 0)
         gate_half(1, 1)
         linear_half(0, 0, False)
         linear_half(0, 1, False)
+        gather_last(2)
+        gather_words(3, 1)
         linear_half(1, 0, False)
         linear_half(1, 1, False)
+        gather_last(3)
+        turn(0, 0, 2)
         gate_half(2, 0)
         gate_half(2, 1)
-        gate_half(3, 0)
-        gate_half(3, 1)
-        turn(0, 0, 2)
-        turn(1, 0, 2)
         linear_half(2, 0, False)
         linear_half(2, 1, False)
+        gate_half(3, 0)
+        gate_half(3, 1)
         linear_half(3, 0, False)
         linear_half(3, 1, True)
+        turn(1, 0, 2)
         turn(2, 0, 2)
         turn(3, 0, 1)
         turn(3, 1, 1)

@@ -41,7 +41,8 @@ def tile_moe_hot_glu_gelu_kernel(
 
         xw = [keep.tile([P, T], I32, name=f"xw{s}", align_bytes=AL) for s in range(PASSES)]
         xs_both = keep.tile([P, T], U8, align_bytes=AL)
-        xs_last = keep.tile([P, T], U8, align_bytes=AL)
+        xs_last = keep.tile([P, COLD * C], U8, align_bytes=AL)
+        gs_cold = keep.tile([P, COLD * C], U8, align_bytes=AL)
         wh_pair = [keep.tile([P, HOT, PASSES, H], I32, name=f"wh{m}", align_bytes=AL) for m in range(2)]
         wh = [[wh_pair[m][:, e] for e in range(HOT)] for m in range(2)]
         wc = [keep.tile([P, COLD * PASSES, 2 * H], U8, name=f"wc{m}", align_bytes=AL) for m in range(2)]
@@ -120,16 +121,17 @@ def tile_moe_hot_glu_gelu_kernel(
             nc.vector.tensor_copy(gw[e, s][:], xw[s][:].bitcast(U32).indirect(picks(e)))
 
         def gather_scales(e):
-            both = gathered[tile_of[f"S{e}"]]
-            nc.vector.tensor_copy(both[:], xs_both[:].indirect(picks(e)))
-            gs[e, 0] = both[:]
             if e < HOT:
+                both = gathered[tile_of[f"S{e}"]][:]
                 gs[e, 1] = both[4:P, :]
+            else:
+                both = gs_cold[:, (e - HOT) * C : (e - HOT + 1) * C]
+                gs[e, 1] = xs_last[:, (e - HOT) * C : (e - HOT + 1) * C]
+            nc.vector.tensor_copy(both, xs_both[:].indirect(picks(e)))
+            gs[e, 0] = both
 
-        def gather_last(e):
-            last = gathered[{"B2":"S0","B3":"S1"}[f"B{e}"]]
-            nc.vector.tensor_copy(last[:], xs_last[:].indirect(picks(e)))
-            gs[e, 1] = last[:]
+        def move_last_pass_scales(eng, q):
+            eng.dma_start(xs_last[quad_rows(q, 4), :].bitcast(I32), gs_cold[32 * q + 4 : 32 * q + 8, :].bitcast(I32))
 
         def first_layer(m, e, t):
             cols = slice(t * P, (t + 1) * P)
@@ -205,6 +207,17 @@ def tile_moe_hot_glu_gelu_kernel(
         nc.sync.dma_start(xs_both[quad_rows(3, 8), :].bitcast(I32), x_scales[:, blocks(3), :].bitcast(I32))
         nc.sync.dma_start(offs_t[:], offs)
         nc.sync.dma_start(xw[1][:], x_words[1].rearrange("p t d -> p (t d)").bitcast(I32))
+        gather_words(0, 0)
+        gather_scales(0)
+        gather_words(1, 0)
+        gather_scales(1)
+        gather_words(0, 1)
+        gather_words(1, 1)
+        gather_scales(2)
+        gather_scales(3)
+        gather_words(2, 0)
+        gather_words(2, 1)
+        gather_words(3, 0)
         load_hot_pass(nc.sync, 0, 0)
         load_packed(nc.sync, sh[0], w1h_scales, 0)
         load_packed(nc.sync, sh[0], w1h_scales, 1)
@@ -217,20 +230,20 @@ def tile_moe_hot_glu_gelu_kernel(
         load_packed(nc.sync, sh[1], w3h_scales, 2)
         load_packed(nc.sync, sh[1], w3h_scales, 3)
         load_hot(nc.sync, 1, 1)
-        nc.gpsimd.dma_start(xs_last[quad_rows(0, 4), :].bitcast(I32), x_scales[1, blocks(0), :].bitcast(I32))
-        nc.gpsimd.dma_start(xs_last[quad_rows(1, 4), :].bitcast(I32), x_scales[1, blocks(1), :].bitcast(I32))
-        nc.gpsimd.dma_start(xs_last[quad_rows(2, 4), :].bitcast(I32), x_scales[1, blocks(2), :].bitcast(I32))
-        nc.gpsimd.dma_start(xs_last[quad_rows(3, 4), :].bitcast(I32), x_scales[1, blocks(3), :].bitcast(I32))
         load_side(nc.sync, sc[0], w1c_scales, 0)
         load_side(nc.sync, sc[0], w1c_scales, 1)
         load_side(nc.sync, sc[0], w1c_scales, 2)
         load_side(nc.sync, sc[0], w1c_scales, 3)
         load_cold_one(nc.sync, 0, 0)
+        move_last_pass_scales(nc.sync, 0)
+        move_last_pass_scales(nc.sync, 1)
+        move_last_pass_scales(nc.sync, 2)
+        move_last_pass_scales(nc.sync, 3)
         load_cold_one(nc.sync, 1, 0)
-        load_side(nc.sync, sc[1], w3c_scales, 0)
-        load_side(nc.sync, sc[1], w3c_scales, 1)
-        load_side(nc.sync, sc[1], w3c_scales, 2)
-        load_side(nc.sync, sc[1], w3c_scales, 3)
+        load_side(nc.gpsimd, sc[1], w3c_scales, 0)
+        load_side(nc.gpsimd, sc[1], w3c_scales, 1)
+        load_side(nc.gpsimd, sc[1], w3c_scales, 2)
+        load_side(nc.gpsimd, sc[1], w3c_scales, 3)
         load_cold_one(nc.sync, 0, 1)
         load_cold_one(nc.sync, 1, 1)
         nc.sync.dma_start(w2h[:], w2h_words.rearrange("e s p n d -> p (e s) (n d)").bitcast(I32))
@@ -246,28 +259,15 @@ def tile_moe_hot_glu_gelu_kernel(
         nc.sync.dma_start(pos_t[0][:], pos1)
         nc.sync.dma_start(gate_t[:], gate.rearrange("r p t -> p r t"))
         nc.sync.dma_start(pos_t[1][:], pos2)
-        gather_words(0, 0)
-        gather_scales(0)
-        gather_words(1, 0)
-        gather_scales(1)
-        gather_words(0, 1)
-        gather_words(1, 1)
-        gather_words(2, 0)
-        gather_scales(2)
-        gather_words(2, 1)
-        gather_words(3, 0)
-        gather_scales(3)
         gate_half(0, 0)
         gate_half(0, 1)
         gate_half(1, 0)
         gate_half(1, 1)
         linear_half(0, 0, False)
         linear_half(0, 1, False)
-        gather_last(2)
         gather_words(3, 1)
         linear_half(1, 0, False)
         linear_half(1, 1, False)
-        gather_last(3)
         turn(0, 0, 2)
         gate_half(2, 0)
         gate_half(2, 1)

from contextlib import ExitStack

import concourse.mybir as mybir
from concourse.masks import make_identity

K, T, E, C, H, N, HOT = 1024, 512, 4, 256, 512, 128, 2
FLOPS = 2 * E * C * (2 * K * H + H * N)

F32 = mybir.dt.float32
BF16 = mybir.dt.bfloat16
I32 = mybir.dt.int32
U32 = mybir.dt.uint32
U16 = mybir.dt.uint16
U8 = mybir.dt.uint8
FP8X4 = mybir.dt.float8_e4m3fn_x4
FP4X4 = mybir.dt.float4_e2m1fn_x4
MULT = mybir.AluOpType.mult
ADD = mybir.AluOpType.add
GELU = mybir.ActivationFunctionType.Gelu_apprx_tanh

P = 128
PASSES = 2
COLD = E - HOT
QUADS = 4
AL = 64


def tile_moe_hot_glu_gelu_kernel(
    tc, x_words, x_scales, w1h_words, w1h_scales, w3h_words, w3h_scales, w2h_words, w2h_scales,
    w1c_words, w1c_scales, w3c_words, w3c_scales, w2c_words, w2c_scales, gate, offs, pos1, pos2, out,
):
    nc = tc.nc
    with ExitStack() as ctx:
        lists = ctx.enter_context(tc.tile_pool(name="lists", bufs=1))
        keep = ctx.enter_context(tc.tile_pool(name="keep", bufs=1))
        work = ctx.enter_context(tc.tile_pool(name="work", bufs=3))
        psum = ctx.enter_context(tc.psum_pool(name="psum", bufs=1))

        offs_t = lists.tile([P, E * C // 16], U16, name="offs_t")
        pos_t = [lists.tile([P, T // 16], U16, name=f"pos_t{r}") for r in range(2)]

        xw = [keep.tile([P, T], I32, name=f"xw{s}", align_bytes=AL) for s in range(PASSES)]
        xs_both = keep.tile([P, T], U8, align_bytes=AL)
        xs_last = keep.tile([P, COLD * C], U8, align_bytes=AL)
        gs_cold = keep.tile([P, COLD * C], U8, align_bytes=AL)
        wh_pair = [keep.tile([P, HOT, PASSES, H], I32, name=f"wh{m}", align_bytes=AL) for m in range(2)]
        wh = [[wh_pair[m][:, e] for e in range(HOT)] for m in range(2)]
        wc = [keep.tile([P, COLD * PASSES, 2 * H], U8, name=f"wc{m}", align_bytes=AL) for m in range(2)]
        sh_pair = keep.tile([P, 2, H], U8, align_bytes=AL)
        sh = [sh_pair[:, m, :] for m in range(2)]
        sc_pair = keep.tile([P, 2, COLD * PASSES, H], U8, align_bytes=AL)
        sc = [sc_pair[:, m] for m in range(2)]
        w2h = keep.tile([P, HOT, N], I32, align_bytes=AL)
        w2c = keep.tile([P, COLD, 2 * N], U8, align_bytes=AL)
        s2 = keep.tile([P, 1 + COLD, N], U8, align_bytes=AL)
        s2h, s2c = s2[:, 0, :], s2[:, 1:, :]
        gate_t = keep.tile([P, 2, T], F32, align_bytes=AL)
        ident = keep.tile([P, P], F32, align_bytes=AL)
        y_all = keep.tile([P, E * C], F32, align_bytes=AL)
        warm = keep.tile([P, 8], F32, align_bytes=AL)
        warm_out = keep.tile([P, 8], F32, align_bytes=AL)

        nc.gpsimd.memset(xs_both[:].bitcast(I32), 0)
        nc.gpsimd.memset(sh_pair[:].bitcast(I32), 0)
        nc.vector.memset(warm[:], 0.0)
        nc.vector.memset(xs_last[:].bitcast(I32), 0)
        nc.vector.memset(sc_pair[:].bitcast(I32), 0)
        nc.vector.memset(s2[:].bitcast(I32), 0)

        def quad_rows(q, n):
            return slice(32 * q, 32 * q + n)

        def blocks(q):
            return slice(4 * q, 4 * q + 4)

        def load_packed(eng, plane, scales, q):
            src = scales.rearrange("e s b i -> (e s) b i")
            eng.dma_start(plane[quad_rows(q, 4 * src.shape[0]), :].bitcast(I32), src[:, blocks(q), :].bitcast(I32))

        def load_side(eng, plane, scales, r):
            src = scales.rearrange("e s (q r) i -> r q (e s) i", r=4)
            eng.dma_start(plane[r:P:32, :, :].bitcast(I32), src[r].bitcast(I32))

        def load_hot(eng, m, e):
            src = (w1h_words, w3h_words)[m][e].rearrange("s p i d -> p s (i d)")
            eng.dma_start(wh[m][e][:], src.bitcast(I32))

        def load_cold(eng, m):
            src = (w1c_words, w3c_words)[m].rearrange("f s p c -> p (f s) c")
            eng.dma_start(wc[m][:].bitcast(I32), src.bitcast(I32))

        def load_cold_one(eng, m, f):
            src = (w1c_words, w3c_words)[m][f].rearrange("s p c -> p s c")
            eng.dma_start(wc[m][:, PASSES * f : PASSES * (f + 1), :].bitcast(I32), src.bitcast(I32))

        def load_hot_pass(eng, m, s):
            src = (w1h_words, w3h_words)[m][:, s].rearrange("e p i d -> p e (i d)")
            eng.dma_start(wh_pair[m][:, :, s, :], src.bitcast(I32))

        banks = [psum.tile([P, H], F32, name=f"bank{b}") for b in range(8)]
        bank_of = {"a00":0,"a01":1,"a10":2,"a11":3,"b00":4,"b01":5,"b10":6,"b11":7,"T00":3,"a20":0,"a21":1,"b20":2,"b21":4,"a30":5,"a31":3,"T10":5,"b30":6,"b31":7,"T20":0,"T30":1,"T31":3,"y00":2,"y10":4,"y20":5,"y30":6,"y31":0}
        tile_of = {"W00":"W00","W01":"W01","S0":"S0","W10":"W10","W11":"W11","S1":"S1","W20":"W20","W21":"W21","S2":"S2","W30":"W30","W31":"W01","S3":"S3"}
        gathered = {}
        for name in sorted(set(tile_of.values())):
            gathered[name] = keep.tile([P, C], U32 if name.startswith("W") else U8, name=f"g{name}", align_bytes=AL)
        on_vector = []

        def evacuate(key, dst, src):
            if key in on_vector:
                nc.vector.tensor_copy(dst, src)
            else:
                nc.scalar.copy(dst, src)

        gw, gs, act, h, hq, hscale = {}, {}, {}, {}, {}, {}

        def picks(e):
            return offs_t[:, e * C // 16 : (e + 1) * C // 16]

        def gather_words(e, s):
            gw[e, s] = gathered[tile_of[f"W{e}{s}"]]
            nc.vector.tensor_copy(gw[e, s][:], xw[s][:].bitcast(U32).indirect(picks(e)))

        def gather_scales(e):
            if e < HOT:
                both = gathered[tile_of[f"S{e}"]][:]
                gs[e, 1] = both[4:P, :]
            else:
                both = gs_cold[:, (e - HOT) * C : (e - HOT + 1) * C]
                gs[e, 1] = xs_last[:, (e - HOT) * C : (e - HOT + 1) * C]
            nc.vector.tensor_copy(both, xs_both[:].indirect(picks(e)))
            gs[e, 0] = both

        def move_last_pass_scales(eng, q):
            eng.dma_start(xs_last[quad_rows(q, 4), :].bitcast(I32), gs_cold[32 * q + 4 : 32 * q + 8, :].bitcast(I32))

        def first_layer(m, e, t):
            cols = slice(t * P, (t + 1) * P)
            bank = banks[bank_of["ab"[m] + f"{e}{t}"]]
            for s in range(PASSES):
                if e < HOT:
                    rhs = wh[m][e][:, s, :].bitcast(FP8X4)
                    rhs_scale = sh[m][4 * (PASSES * e + s) : P, :]
                else:
                    rhs = wc[m][:, PASSES * (e - HOT) + s, :].bitcast(FP4X4)
                    rhs_scale = sc[m][:, PASSES * (e - HOT) + s, :]
                nc.tensor.matmul_mx(
                    out=bank[:], lhsT=gw[e, s][:, cols].bitcast(FP8X4), lhsT_scale=gs[e, s][:, cols],
                    rhs=rhs, rhs_scale=rhs_scale, start=(s == 0), stop=(s == PASSES - 1),
                )
            return bank[:].rearrange("j (p u v) -> j u p v", u=2, v=2)

        def gate_half(e, t):
            act[e, t] = work.tile([P, 2, P, 2], F32, name="act", align_bytes=AL, bufs=8)
            nc.scalar.activation(act[e, t][:], first_layer(0, e, t), GELU)

        def linear_half(e, t, halves):
            lin = first_layer(1, e, t)
            h[e, t] = work.tile([P, 2, P, 2], BF16, name="h", align_bytes=AL, bufs=8)
            if halves:
                for u in range(2):
                    nc.vector.tensor_tensor(h[e, t][:, u], lin[:, u], act[e, t][:, u], MULT)
            else:
                nc.vector.tensor_tensor(h[e, t][:], lin, act[e, t][:], MULT)

        def linear_half_pool(e, t):
            lin = work.tile([P, 2, P, 2], F32, name="lin", align_bytes=AL, bufs=4)
            nc.scalar.copy(lin[:], first_layer(1, e, t))
            h[e, t] = work.tile([P, 2, P, 2], BF16, name="h", align_bytes=AL, bufs=8)
            flat = "j u p v -> j (u p v)"
            nc.gpsimd.tensor_tensor(h[e, t][:].rearrange(flat), lin[:].rearrange(flat), act[e, t][:].rearrange(flat), MULT)

        def turn(e, t0, n):
            bank = banks[bank_of[f"T{e}{t0}"]][:].rearrange("p (t u j) -> p t u j", t=2, u=2)
            for t in range(n):
                for u in range(2):
                    words = h[e, t0 + t][:, u].rearrange("j p v -> j (p v)").bitcast(F32)
                    nc.tensor.transpose(bank[:, t, u, :], words, ident[:])
            ht = work.tile([P, n * P * 4], BF16, name="ht", align_bytes=AL, bufs=5)
            evacuate(
                f"ct{e}{t0}",
                ht[:].bitcast(F32).rearrange("p (t j u) -> p t j u", t=n, u=2),
                bank[:, 0:n].rearrange("p t u j -> p t j u"),
            )
            hq[e, t0] = work.tile([P, n * P], U32, name="hq", align_bytes=AL, bufs=5)
            hscale[e, t0] = work.tile([P, n * P], U8, name="hscale", align_bytes=AL, bufs=5)
            nc.vector.quantize_mx(out=hq[e, t0][:].bitcast(FP8X4), scales=hscale[e, t0][:], in_=ht[:])

        def second_layer(e, t0, n):
            bank = banks[bank_of[f"y{e}{t0}"]][:, 0 : n * P]
            if e < HOT:
                lhsT, lhsT_scale = w2h[:, e, :].bitcast(FP8X4), s2h[4 * e : P, :]
            else:
                lhsT, lhsT_scale = w2c[:, e - HOT, :].bitcast(FP4X4), s2c[:, e - HOT, :]
            nc.tensor.matmul_mx(
                out=bank, lhsT=lhsT, lhsT_scale=lhsT_scale,
                rhs=hq[e, t0][:].bitcast(FP8X4), rhs_scale=hscale[e, t0][:], start=True, stop=True,
            )
            slot0 = e * C + t0 * P
            evacuate(f"cy{e}{t0}", y_all[:, slot0 : slot0 + n * P], bank)

        make_identity(nc, ident[:])
        nc.scalar.activation(warm_out[:], warm[:], GELU)
        nc.sync.dma_start(xw[0][:], x_words[0].rearrange("p t d -> p (t d)").bitcast(I32))
        nc.sync.dma_start(xs_both[quad_rows(0, 8), :].bitcast(I32), x_scales[:, blocks(0), :].bitcast(I32))
        nc.sync.dma_start(xs_both[quad_rows(1, 8), :].bitcast(I32), x_scales[:, blocks(1), :].bitcast(I32))
        nc.sync.dma_start(xs_both[quad_rows(2, 8), :].bitcast(I32), x_scales[:, blocks(2), :].bitcast(I32))
        nc.sync.dma_start(xs_both[quad_rows(3, 8), :].bitcast(I32), x_scales[:, blocks(3), :].bitcast(I32))
        nc.sync.dma_start(offs_t[:], offs)
        nc.sync.dma_start(xw[1][:], x_words[1].rearrange("p t d -> p (t d)").bitcast(I32))
        gather_words(0, 0)
        gather_scales(0)
        gather_words(1, 0)
        gather_scales(1)
        gather_words(0, 1)
        gather_words(1, 1)
        gather_scales(2)
        gather_scales(3)
        gather_words(2, 0)
        gather_words(2, 1)
        gather_words(3, 0)
        load_hot_pass(nc.sync, 0, 0)
        load_packed(nc.sync, sh[0], w1h_scales, 0)
        load_packed(nc.sync, sh[0], w1h_scales, 1)
        load_packed(nc.sync, sh[0], w1h_scales, 2)
        load_packed(nc.sync, sh[0], w1h_scales, 3)
        load_hot_pass(nc.sync, 0, 1)
        load_hot(nc.sync, 1, 0)
        load_packed(nc.sync, sh[1], w3h_scales, 0)
        load_packed(nc.sync, sh[1], w3h_scales, 1)
        load_packed(nc.sync, sh[1], w3h_scales, 2)
        load_packed(nc.sync, sh[1], w3h_scales, 3)
        load_hot(nc.sync, 1, 1)
        load_side(nc.sync, sc[0], w1c_scales, 0)
        load_side(nc.sync, sc[0], w1c_scales, 1)
        load_side(nc.sync, sc[0], w1c_scales, 2)
        load_side(nc.sync, sc[0], w1c_scales, 3)
        load_cold_one(nc.sync, 0, 0)
        move_last_pass_scales(nc.sync, 0)
        move_last_pass_scales(nc.sync, 1)
        move_last_pass_scales(nc.sync, 2)
        move_last_pass_scales(nc.sync, 3)
        load_cold_one(nc.sync, 1, 0)
        load_side(nc.gpsimd, sc[1], w3c_scales, 0)
        load_side(nc.gpsimd, sc[1], w3c_scales, 1)
        load_side(nc.gpsimd, sc[1], w3c_scales, 2)
        load_side(nc.gpsimd, sc[1], w3c_scales, 3)
        load_cold_one(nc.sync, 0, 1)
        load_cold_one(nc.sync, 1, 1)
        nc.sync.dma_start(w2h[:], w2h_words.rearrange("e s p n d -> p (e s) (n d)").bitcast(I32))
        load_packed(nc.sync, s2h, w2h_scales, 0)
        load_packed(nc.sync, s2h, w2h_scales, 1)
        load_packed(nc.sync, s2h, w2h_scales, 2)
        load_packed(nc.sync, s2h, w2h_scales, 3)
        nc.sync.dma_start(w2c[:].bitcast(I32), w2c_words.rearrange("f s p c -> p (f s) c").bitcast(I32))
        load_side(nc.sync, s2c, w2c_scales, 0)
        load_side(nc.sync, s2c, w2c_scales, 1)
        load_side(nc.sync, s2c, w2c_scales, 2)
        load_side(nc.sync, s2c, w2c_scales, 3)
        nc.sync.dma_start(pos_t[0][:], pos1)
        nc.sync.dma_start(gate_t[:], gate.rearrange("r p t -> p r t"))
        nc.sync.dma_start(pos_t[1][:], pos2)
        gate_half(0, 0)
        gate_half(0, 1)
        gate_half(1, 0)
        gate_half(1, 1)
        linear_half(0, 0, False)
        linear_half(0, 1, False)
        gather_words(3, 1)
        linear_half(1, 0, False)
        linear_half(1, 1, False)
        turn(0, 0, 2)
        gate_half(2, 0)
        gate_half(2, 1)
        linear_half(2, 0, False)
        linear_half(2, 1, False)
        gate_half(3, 0)
        gate_half(3, 1)
        linear_half(3, 0, False)
        linear_half(3, 1, True)
        turn(1, 0, 2)
        turn(2, 0, 2)
        turn(3, 0, 1)
        turn(3, 1, 1)
        second_layer(0, 0, 2)
        second_layer(1, 0, 2)
        second_layer(2, 0, 2)
        second_layer(3, 0, 1)
        second_layer(3, 1, 1)

        half = T // 2
        first_part = keep.tile([P, T], F32, align_bytes=AL)
        nc.vector.tensor_tensor(first_part[:], y_all[:].indirect(pos_t[0][:]), gate_t[:, 0, :], MULT)
        second_part = keep.tile([P, T], F32, align_bytes=AL)
        total = keep.tile([P, T], F32, align_bytes=AL)
        for c in range(2):
            cols = slice(c * half, (c + 1) * half)
            nc.vector.tensor_tensor(
                second_part[:, cols], y_all[:].indirect(pos_t[1][:, c * half // 16 : (c + 1) * half // 16]),
                gate_t[:, 1, cols], MULT,
            )
        for c in range(2):
            cols = slice(c * half, (c + 1) * half)
            nc.vector.tensor_tensor(total[:, cols], first_part[:, cols], second_part[:, cols], ADD)
            nc.sync.dma_start(out[:, cols], total[:, cols])
